import numpy as np
import ml_dtypes


def mxq(x, axis, fmt="e4m3"):
    dtype, down = {"e4m3": (ml_dtypes.float8_e4m3fn, 7), "e5m2": (ml_dtypes.float8_e5m2, 14)}[fmt]
    v = np.moveaxis(np.asarray(x, np.float32).astype(ml_dtypes.bfloat16).astype(np.float64), axis, -1)
    blocks = v.reshape(v.shape[:-1] + (-1, 32))
    amax = np.abs(blocks).max(-1, keepdims=True)
    byte = np.maximum(np.where(amax > 0, np.frexp(amax)[1] - 1 + 127, 0) - down, 1)
    scale = np.exp2(byte - 127.0)
    codes = (blocks / scale).astype(np.float32).astype(dtype).astype(np.float64)
    return np.moveaxis((codes * scale).reshape(v.shape), -1, axis)


WIDE = False


def mx_kscale(k):
    if not WIDE:
        return np.ones(k)
    levels = np.array([10, -10, 5, -5, 0])
    if k % 512:
        return np.exp2(np.random.permutation(np.resize(levels, k // 32))).repeat(32)
    a = np.empty((k // 512, 16))
    for p in range(k // 512):
        a[p, :8] = np.random.permutation(np.resize(levels, 8))
        for g in range(8):
            far = levels[np.abs(levels - a[p, g]) >= 10]
            a[p, g + 8] = far[np.random.randint(len(far))]
    return np.exp2(a.ravel()).repeat(32)


def f64(x):
    return np.asarray(x).astype(np.float64)


def striped8(idx):
    return np.asarray(idx).reshape(8, -1, 16).transpose(0, 2, 1).reshape(128, -1).astype(np.uint16)


def unstriped8(offs):
    return offs.reshape(8, 16, -1).transpose(0, 2, 1).reshape(8, -1).astype(np.int64)


def pick8(x, idx, run):
    r = np.arange(len(x))
    return x[r[:, None], idx[r % (8 * run) // run]]


E2M1 = np.array([0.0, 0.5, 1.0, 1.5, 2.0, 3.0, 4.0, 6.0, -0.0, -0.5, -1.0, -1.5, -2.0, -3.0, -4.0, -6.0])


def pack_weight(w, fmt):
    k, n = w.shape
    w = f64(np.asarray(w, np.float32).astype(ml_dtypes.bfloat16)).reshape(k // 32, 32, n)
    amax = np.abs(w).max(1)
    if fmt == "e4m3":
        byte = np.frexp(amax)[1] - 1 + 127 - 7
    else:
        mant, ex = np.frexp(amax / 6.0)
        byte = np.where(mant > 0.5, ex, ex - 1) + 127
    byte = np.clip(np.where(amax > 0, byte, 1), 1, 254)
    scaled = (w * np.exp2(127.0 - byte)[:, None, :]).reshape(k, n).astype(np.float32)
    by_word = np.ascontiguousarray(scaled.reshape(k // 512, 128, 4, n).transpose(0, 1, 3, 2))
    if fmt == "e4m3":
        words = by_word.astype(ml_dtypes.float8_e4m3fn).view(np.uint8)
    else:
        c = by_word.astype(ml_dtypes.float4_e2m1fn).view(np.uint8) & 0xF
        words = (c[..., 0::2] | (c[..., 1::2] << 4)).reshape(k // 512, 128, 2 * n)
    return np.ascontiguousarray(words), np.ascontiguousarray(byte.astype(np.uint8).reshape(k // 512, 16, n))


def unpack_weight(words, scales, fmt):
    g, _, n = scales.shape
    words = np.ascontiguousarray(words).reshape(g, 128, n, -1)
    if fmt == "e4m3":
        vals = words.view(ml_dtypes.float8_e4m3fn).astype(np.float64)
    else:
        nib = np.empty((g, 128, n, 4), np.uint8)
        nib[..., 0::2] = words & 0xF
        nib[..., 1::2] = words >> 4
        vals = E2M1[nib]
    vals = vals * np.repeat(np.exp2(scales.astype(np.float64) - 127.0), 8, axis=1)[..., None]
    return vals.transpose(0, 1, 3, 2).reshape(g * 512, n)


D, E, T, Q, I = 512, 512, 1024, 128, 256


def setup_inputs():
    n = np.random.standard_normal
    idx = np.stack([np.random.permutation(T)[:I] for _ in range(8)])
    fd = mx_kscale(D)
    fe = mx_kscale(E)
    keysp = pack_weight(n((D, T)) / fd[:, None], "e4m3")
    return {
        "query": (n((D, Q)) * 0.6 / np.sqrt(D) * fd[:, None]).astype(np.float32),
        "keys_words": keysp[0],
        "keys_scales": keysp[1],
        "gout": (n((E, Q)) * 1 / np.sqrt(E) * fe[:, None]).astype(np.float32),
        "vals": (n((E, T)) / fe[:, None]).astype(np.float32),
        "zp": (np.random.uniform(200.0, 800.0, (Q, 1))).astype(np.float32),
        "cp": (np.random.uniform(-100.0, 100.0, (Q, 1))).astype(np.float32),
        "dquery": (n((D, Q)) * 1.0 / np.sqrt(D) * fd[:, None]).astype(np.float32),
        "base": (0.5 * n((Q, T))).astype(np.float32),
        "offs": striped8(idx),
    }


def reference(query, keys_words, keys_scales, gout, vals, zp, cp, dquery, base, offs):
    idx = unstriped8(offs)
    keysu = unpack_weight(keys_words, keys_scales, "e4m3")
    queryq = mxq(f64(query), 0, "e4m3")
    a = queryq.T @ keysu
    dqueryq = mxq(f64(dquery), 0, "e4m3")
    ta = dqueryq.T @ keysu
    p = np.exp(pick8(a, idx, 16))
    z = np.sum(p, axis=1, keepdims=True) + f64(zp)
    goutq = mxq(f64(gout), 0, "e4m3")
    valsq = mxq(f64(vals), 0, "e4m3")
    c0 = goutq.T @ valsq
    dz = (np.sum(p * pick8(c0, idx, 16), axis=1, keepdims=True) + f64(cp)) / np.square(z) * (-1.0)
    dp = 1.0 / z * pick8(c0, idx, 16) + dz
    xp = pick8(ta, idx, 16) * p
    xz = np.sum(xp, axis=1, keepdims=True)
    xdz = (np.sum(xp * pick8(c0, idx, 16), axis=1, keepdims=True) - xz * z * 2.0 * (np.sum(p * pick8(c0, idx, 16), axis=1, keepdims=True) + f64(cp)) / np.square(z)) / np.square(z) * (-1.0)
    xdp = xz * 1.0 / np.square(z) * (-1.0) * pick8(c0, idx, 16) + xdz
    xe1 = xdp * p + xp * dp
    xs1 = np.zeros((Q, T))
    xs1[np.arange(Q)[:, None], idx[np.arange(Q) % 128 // 16]] = xe1
    y = xs1 * 1024.0 + f64(base)
    return y

@@ -1,0 +1,158 @@
+from contextlib import ExitStack
+
+import concourse.mybir as mybir
+
+D, E, T, Q, SLOTS = 512, 512, 1024, 128, 256
+FLOPS = 3 * 2 * 512 * Q * T
+
+F32 = mybir.dt.float32
+BF16 = mybir.dt.bfloat16
+I32 = mybir.dt.int32
+U32 = mybir.dt.uint32
+U16 = mybir.dt.uint16
+U8 = mybir.dt.uint8
+FP8X4 = mybir.dt.float8_e4m3fn_x4
+ALU = mybir.AluOpType
+ACT = mybir.ActivationFunctionType
+
+P = 128
+PACK = 4
+BANK = 512
+PAD = 8
+VALS_CHUNKS = (512, 256, 128, 128)
+SCALAR_COLS = (128, 128, 0, 0)
+STORE_COLS = 256
+
+
+def tile_attend_hvsharedprefix_heads_kernel(tc, query, keys_words, keys_scales, gout, vals, zp, cp, dquery, base, offs, out):
+    nc = tc.nc
+    with ExitStack() as ctx:
+        sb = ctx.enter_context(tc.tile_pool(name="sb", bufs=1))
+        ps = ctx.enter_context(tc.psum_pool(name="ps", bufs=1))
+
+        def load_rows(name, rows):
+            raw = sb.tile([P, PACK, rows.shape[1]], F32, name=name + "_raw", align_bytes=64)
+            nc.sync.dma_start(out=raw[:], in_=rows.rearrange("(p j) w -> p j w", j=PACK))
+            return raw
+
+        def interleave(copy, grouped, raw, c0, c1):
+            copy(
+                grouped[:, c0:c1, :].rearrange("p (c i) j -> p c j i", i=4),
+                raw[:, :, c0:c1].rearrange("p j (c i) -> p c j i", i=4),
+            )
+
+        def quantise(name, raw, scalar_cols):
+            width = raw.shape[2]
+            grouped = sb.tile([P, width, PACK], BF16, name=name + "_bf16", align_bytes=64)
+            codes = sb.tile([P, width], U32, name=name + "_codes", align_bytes=64)
+            scales = sb.tile([P, width], U8, name=name + "_scales", align_bytes=64)
+            split = width - scalar_cols
+            if split > 0:
+                interleave(nc.vector.tensor_copy, grouped, raw, 0, split)
+            if scalar_cols > 0:
+                interleave(nc.scalar.copy, grouped, raw, split, width)
+            nc.vector.quantize_mx(out=codes[:].bitcast(FP8X4), scales=scales[:], in_=grouped[:].rearrange("p w j -> p (w j)"))
+            return codes, scales
+
+        def product(name, lhs, rhs, cols):
+            bank = ps.tile([P, BANK], F32, name=name)
+            width = cols.stop - cols.start
+            nc.tensor.matmul_mx(
+                out=bank[:, :width],
+                lhsT=lhs[0][:].bitcast(FP8X4),
+                lhsT_scale=lhs[1][:],
+                rhs=rhs[0][:, cols].bitcast(FP8X4),
+                rhs_scale=rhs[1][:, cols],
+                start=True,
+                stop=True,
+            )
+            return bank[:, :width]
+
+        key_codes = sb.tile([P, T], U32, name="key_codes", align_bytes=64)
+        key_scales = sb.tile([P, T], U8, name="key_scales", align_bytes=64)
+        offsets = sb.tile([P, SLOTS // 16], U16, name="offsets")
+        p_ext = sb.tile([P, PAD + SLOTS + PAD], F32, name="p_ext", align_bytes=64)
+        t_ext = sb.tile([P, SLOTS + PAD], F32, name="t_ext", align_bytes=64)
+        c_ext = sb.tile([P, SLOTS + PAD], F32, name="c_ext", align_bytes=64)
+        placed = sb.tile([P, T], F32, name="placed", align_bytes=64)
+
+        nc.vector.memset(key_scales[:].bitcast(I32), 0)
+        nc.vector.memset(t_ext[:, SLOTS : SLOTS + 1], 0.0)
+        nc.scalar.activation(c_ext[:, SLOTS : SLOTS + 1], t_ext[:, SLOTS : SLOTS + 1], ACT.Exp)
+        nc.vector.memset(placed[:], 0.0)
+
+        nc.sync.dma_start(offsets[:], offs)
+        query_raw = load_rows("query", query)
+        for r in range(4):
+            nc.sync.dma_start(out=key_scales[r:P:32, :].bitcast(I32), in_=keys_scales[0, r:16:4, :].bitcast(I32))
+        nc.sync.dma_start(out=key_codes[:].bitcast(I32), in_=keys_words[0].rearrange("p n t -> p (n t)").bitcast(I32))
+        dquery_raw = load_rows("dquery", dquery)
+        gout_raw = load_rows("gout", gout)
+        vals_raw = []
+        start = 0
+        for n, width in enumerate(VALS_CHUNKS):
+            vals_raw.append(load_rows("vals%d" % n, vals[:, start : start + width]))
+            start += width
+        base_sb = sb.tile([P, T], F32, name="base_sb", align_bytes=64)
+        nc.sync.dma_start(out=base_sb[:], in_=base)
+        nc.gpsimd.dma_start(out=p_ext[:, PAD - 1 : PAD], in_=zp)
+        nc.gpsimd.dma_start(out=p_ext[:, PAD + SLOTS : PAD + SLOTS + 1], in_=cp)
+
+        keys = (key_codes, key_scales)
+        halves = [slice(0, BANK), slice(BANK, T)]
+        a_sb = sb.tile([P, T], F32, name="a_sb", align_bytes=64)
+        ta_sb = sb.tile([P, T], F32, name="ta_sb", align_bytes=64)
+        c_sb = sb.tile([P, T], F32, name="c_sb", align_bytes=64)
+
+        query_mx = quantise("query", query_raw, 0)
+        dquery_mx = quantise("dquery", dquery_raw, 0)
+        a_banks = [product("a%d" % h, query_mx, keys, halves[h]) for h in range(2)]
+        ta_banks = [product("ta%d" % h, dquery_mx, keys, halves[h]) for h in range(2)]
+        nc.scalar.copy(a_sb[:, halves[0]], a_banks[0])
+        nc.vector.tensor_copy(a_sb[:, halves[1]], a_banks[1])
+        gout_mx = quantise("gout", gout_raw, 0)
+        p = p_ext[:, PAD : PAD + SLOTS]
+        nc.scalar.activation(p, a_sb[:].indirect(offsets[:]), ACT.Exp)
+        nc.vector.tensor_copy(ta_sb[:, halves[0]], ta_banks[0])
+        nc.scalar.copy(ta_sb[:, halves[1]], ta_banks[1])
+
+        z = sb.tile([P, 1], F32, name="z")
+        z_terms = sb.tile([P, SLOTS + 1], F32, name="z_terms")
+        nc.scalar.activation(z_terms[:], p_ext[:, PAD - 1 : PAD + SLOTS], ACT.Copy, accum_out=z[:])
+        nc.vector.tensor_copy(t_ext[:, :SLOTS], ta_sb[:].indirect(offsets[:]))
+        rz = sb.tile([P, 1], F32, name="rz")
+        nc.vector.reciprocal(rz[:], z[:])
+        s = sb.tile([P, SLOTS + 1], F32, name="s", align_bytes=64)
+        nc.scalar.activation(s[:], p_ext[:, PAD : PAD + SLOTS + 1], ACT.Copy, scale=rz[:])
+        tbar = sb.tile([P, 1], F32, name="tbar")
+        tbar_terms = sb.tile([P, SLOTS], F32, name="tbar_terms")
+        nc.vector.scalar_tensor_tensor(tbar_terms[:], t_ext[:, :SLOTS], rz[:], p, ALU.mult, ALU.mult, accum_out=tbar[:])
+        u = sb.tile([P, SLOTS + 1], F32, name="u", align_bytes=64)
+        nc.vector.scalar_tensor_tensor(u[:], t_ext[:, : SLOTS + 1], tbar[:], s[:], ALU.subtract, ALU.mult)
+
+        start = 0
+        for n, width in enumerate(VALS_CHUNKS):
+            vals_mx = quantise("vals%d" % n, vals_raw[n], SCALAR_COLS[n])
+            bank = product("c%d" % n, gout_mx, vals_mx, slice(0, width))
+            nc.scalar.copy(c_sb[:, start : start + width], bank)
+            start += width
+
+        nc.vector.tensor_copy(c_ext[:, :SLOTS], c_sb[:].indirect(offsets[:]))
+        cbar = sb.tile([P, 1], F32, name="cbar")
+        cbar_terms = sb.tile([P, SLOTS + 1], F32, name="cbar_terms")
+        nc.vector.scalar_tensor_tensor(cbar_terms[:], c_ext[:, : SLOTS + 1], 1.0, s[:], ALU.mult, ALU.mult, accum_out=cbar[:])
+        k = sb.tile([P, 1], F32, name="k")
+        k_terms = sb.tile([P, SLOTS + 1], F32, name="k_terms")
+        nc.vector.scalar_tensor_tensor(k_terms[:], c_ext[:, : SLOTS + 1], -1.0, u[:], ALU.mult, ALU.mult, accum_out=k[:])
+        centred = sb.tile([P, SLOTS], F32, name="centred", align_bytes=64)
+        nc.vector.scalar_tensor_tensor(centred[:], c_ext[:, :SLOTS], cbar[:], u[:, :SLOTS], ALU.subtract, ALU.mult)
+        shift = sb.tile([P, SLOTS], F32, name="shift", align_bytes=64)
+        nc.scalar.activation(shift[:], s[:, :SLOTS], ACT.Copy, scale=k[:])
+        nc.vector.tensor_tensor(placed[:].indirect(offsets[:]), centred[:], shift[:], ALU.add)
+
+        for n in range(T // STORE_COLS):
+            cols = slice(n * STORE_COLS, (n + 1) * STORE_COLS)
+            result = sb.tile([P, STORE_COLS], F32, name="result%d" % n, align_bytes=64)
+            nc.vector.scalar_tensor_tensor(result[:], placed[:, cols], 1024.0, base_sb[:, cols], ALU.mult, ALU.add)
+            queue = nc.sync if n % 2 == 0 else nc.scalar
+            queue.dma_start(out=out[:, cols], in_=result[:])

@@ -19,8 +19,8 @@ P = 128
 PACK = 4
 BANK = 512
 PAD = 8
-VALS_CHUNKS = (512, 256, 128, 128)
-SCALAR_COLS = (128, 128, 0, 0)
+VALS_LOADS = (512, 384, 128)
+VALS_PASSES = ((0, 0, 512, 256), (1, 256, 128, 128), (1, 0, 256, 0), (2, 0, 128, 128))
 STORE_COLS = 256
 
 
@@ -35,23 +35,23 @@ def tile_attend_hvsharedprefix_heads_kernel(tc, query, keys_words, keys_scales, 
             nc.sync.dma_start(out=raw[:], in_=rows.rearrange("(p j) w -> p j w", j=PACK))
             return raw
 
-        def interleave(copy, grouped, raw, c0, c1):
-            copy(
-                grouped[:, c0:c1, :].rearrange("p (c i) j -> p c j i", i=4),
-                raw[:, :, c0:c1].rearrange("p j (c i) -> p c j i", i=4),
-            )
+        def interleave(copy, grouped, raw):
+            copy(grouped.rearrange("p (c i j) -> p c j i", i=4, j=PACK), raw.rearrange("p j (c i) -> p c j i", i=4))
 
-        def quantise(name, raw, scalar_cols):
-            width = raw.shape[2]
-            grouped = sb.tile([P, width, PACK], BF16, name=name + "_bf16", align_bytes=64)
-            codes = sb.tile([P, width], U32, name=name + "_codes", align_bytes=64)
-            scales = sb.tile([P, width], U8, name=name + "_scales", align_bytes=64)
+        def round_to_bf16(name, raw, first, width, scalar_cols):
+            grouped = sb.tile([P, width * PACK], BF16, name=name + "_bf16", align_bytes=64)
             split = width - scalar_cols
             if split > 0:
-                interleave(nc.vector.tensor_copy, grouped, raw, 0, split)
+                interleave(nc.vector.tensor_copy, grouped[:, : split * PACK], raw[:, :, first : first + split])
             if scalar_cols > 0:
-                interleave(nc.scalar.copy, grouped, raw, split, width)
-            nc.vector.quantize_mx(out=codes[:].bitcast(FP8X4), scales=scales[:], in_=grouped[:].rearrange("p w j -> p (w j)"))
+                interleave(nc.scalar.copy, grouped[:, split * PACK :], raw[:, :, first + split : first + width])
+            return grouped
+
+        def quantise(name, grouped):
+            width = grouped.shape[1] // PACK
+            codes = sb.tile([P, width], U32, name=name + "_codes", align_bytes=64)
+            scales = sb.tile([P, width], U8, name=name + "_scales", align_bytes=64)
+            nc.vector.quantize_mx(out=codes[:].bitcast(FP8X4), scales=scales[:], in_=grouped[:])
             return codes, scales
 
         def product(name, lhs, rhs, cols):
@@ -81,78 +81,82 @@ def tile_attend_hvsharedprefix_heads_kernel(tc, query, keys_words, keys_scales, 
         nc.scalar.activation(c_ext[:, SLOTS : SLOTS + 1], t_ext[:, SLOTS : SLOTS + 1], ACT.Exp)
         nc.vector.memset(placed[:], 0.0)
 
-        nc.sync.dma_start(offsets[:], offs)
         query_raw = load_rows("query", query)
         for r in range(4):
             nc.sync.dma_start(out=key_scales[r:P:32, :].bitcast(I32), in_=keys_scales[0, r:16:4, :].bitcast(I32))
         nc.sync.dma_start(out=key_codes[:].bitcast(I32), in_=keys_words[0].rearrange("p n t -> p (n t)").bitcast(I32))
         dquery_raw = load_rows("dquery", dquery)
         gout_raw = load_rows("gout", gout)
+        nc.sync.dma_start(offsets[:], offs)
+        nc.sync.dma_start(out=p_ext[:, PAD - 1 : PAD], in_=zp)
+        nc.sync.dma_start(out=p_ext[:, PAD + SLOTS : PAD + SLOTS + 1], in_=cp)
         vals_raw = []
         start = 0
-        for n, width in enumerate(VALS_CHUNKS):
+        for n, width in enumerate(VALS_LOADS):
             vals_raw.append(load_rows("vals%d" % n, vals[:, start : start + width]))
             start += width
         base_sb = sb.tile([P, T], F32, name="base_sb", align_bytes=64)
         nc.sync.dma_start(out=base_sb[:], in_=base)
-        nc.gpsimd.dma_start(out=p_ext[:, PAD - 1 : PAD], in_=zp)
-        nc.gpsimd.dma_start(out=p_ext[:, PAD + SLOTS : PAD + SLOTS + 1], in_=cp)
 
         keys = (key_codes, key_scales)
         halves = [slice(0, BANK), slice(BANK, T)]
         a_sb = sb.tile([P, T], F32, name="a_sb", align_bytes=64)
         ta_sb = sb.tile([P, T], F32, name="ta_sb", align_bytes=64)
-        c_sb = sb.tile([P, T], F32, name="c_sb", align_bytes=64)
 
-        query_mx = quantise("query", query_raw, 0)
-        dquery_mx = quantise("dquery", dquery_raw, 0)
+        query_mx = quantise("query", round_to_bf16("query", query_raw, 0, Q, 0))
+        dquery_mx = quantise("dquery", round_to_bf16("dquery", dquery_raw, 0, Q, 0))
         a_banks = [product("a%d" % h, query_mx, keys, halves[h]) for h in range(2)]
         ta_banks = [product("ta%d" % h, dquery_mx, keys, halves[h]) for h in range(2)]
+        gout_mx = quantise("gout", round_to_bf16("gout", gout_raw, 0, Q, 0))
         nc.scalar.copy(a_sb[:, halves[0]], a_banks[0])
-        nc.vector.tensor_copy(a_sb[:, halves[1]], a_banks[1])
-        gout_mx = quantise("gout", gout_raw, 0)
+        nc.scalar.copy(a_sb[:, halves[1]], a_banks[1])
         p = p_ext[:, PAD : PAD + SLOTS]
         nc.scalar.activation(p, a_sb[:].indirect(offsets[:]), ACT.Exp)
         nc.vector.tensor_copy(ta_sb[:, halves[0]], ta_banks[0])
-        nc.scalar.copy(ta_sb[:, halves[1]], ta_banks[1])
+        nc.vector.tensor_copy(ta_sb[:, halves[1]], ta_banks[1])
 
         z = sb.tile([P, 1], F32, name="z")
         z_terms = sb.tile([P, SLOTS + 1], F32, name="z_terms")
-        nc.scalar.activation(z_terms[:], p_ext[:, PAD - 1 : PAD + SLOTS], ACT.Copy, accum_out=z[:])
-        nc.vector.tensor_copy(t_ext[:, :SLOTS], ta_sb[:].indirect(offsets[:]))
-        rz = sb.tile([P, 1], F32, name="rz")
+        nc.scalar.activation(z_terms[:], p_ext[:, PAD - 1 : PAD + SLOTS], ACT.Copy, scale=-1.0, accum_out=z[:])
+        s = p_ext[:, PAD : PAD + SLOTS + 1]
+
+        c_banks = []
+        for n, (load, first, width, scalar_cols) in enumerate(VALS_PASSES):
+            grouped = round_to_bf16("vals%d" % n, vals_raw[load], first, width, scalar_cols)
+            if n == 0:
+                nc.vector.tensor_copy(t_ext[:, :SLOTS], ta_sb[:].indirect(offsets[:]))
+            vals_mx = quantise("vals%d" % n, grouped)
+            c_banks.append(product("c%d" % n, gout_mx, vals_mx, slice(0, width)))
+        c_sb = sb.tile([P, T], F32, name="c_sb", tag="vals2_raw", align_bytes=64)
+        for bank, (load, first, width, scalar_cols) in zip(c_banks, VALS_PASSES):
+            start = sum(VALS_LOADS[:load]) + first
+            nc.scalar.copy(c_sb[:, start : start + width], bank)
+
+        rz = sb.tile([P, 1], F32, name="rz", tag="vals0_bf16", align_bytes=64)
         nc.vector.reciprocal(rz[:], z[:])
-        s = sb.tile([P, SLOTS + 1], F32, name="s", align_bytes=64)
-        nc.scalar.activation(s[:], p_ext[:, PAD : PAD + SLOTS + 1], ACT.Copy, scale=rz[:])
         tbar = sb.tile([P, 1], F32, name="tbar")
         tbar_terms = sb.tile([P, SLOTS], F32, name="tbar_terms")
         nc.vector.scalar_tensor_tensor(tbar_terms[:], t_ext[:, :SLOTS], rz[:], p, ALU.mult, ALU.mult, accum_out=tbar[:])
-        u = sb.tile([P, SLOTS + 1], F32, name="u", align_bytes=64)
-        nc.vector.scalar_tensor_tensor(u[:], t_ext[:, : SLOTS + 1], tbar[:], s[:], ALU.subtract, ALU.mult)
-
-        start = 0
-        for n, width in enumerate(VALS_CHUNKS):
-            vals_mx = quantise("vals%d" % n, vals_raw[n], SCALAR_COLS[n])
-            bank = product("c%d" % n, gout_mx, vals_mx, slice(0, width))
-            nc.scalar.copy(c_sb[:, start : start + width], bank)
-            start += width
-
+        u = sb.tile([P, SLOTS + 1], F32, name="u", tag="vals3_bf16", align_bytes=64)
+        nc.vector.scalar_tensor_tensor(u[:], t_ext[:, : SLOTS + 1], tbar[:], s, ALU.add, ALU.mult)
         nc.vector.tensor_copy(c_ext[:, :SLOTS], c_sb[:].indirect(offsets[:]))
         cbar = sb.tile([P, 1], F32, name="cbar")
         cbar_terms = sb.tile([P, SLOTS + 1], F32, name="cbar_terms")
-        nc.vector.scalar_tensor_tensor(cbar_terms[:], c_ext[:, : SLOTS + 1], 1.0, s[:], ALU.mult, ALU.mult, accum_out=cbar[:])
+        nc.vector.scalar_tensor_tensor(cbar_terms[:], c_ext[:, : SLOTS + 1], rz[:], s, ALU.mult, ALU.mult, accum_out=cbar[:])
         k = sb.tile([P, 1], F32, name="k")
         k_terms = sb.tile([P, SLOTS + 1], F32, name="k_terms")
-        nc.vector.scalar_tensor_tensor(k_terms[:], c_ext[:, : SLOTS + 1], -1.0, u[:], ALU.mult, ALU.mult, accum_out=k[:])
+        nc.vector.scalar_tensor_tensor(k_terms[:], c_ext[:, : SLOTS + 1], rz[:], u[:], ALU.mult, ALU.mult, accum_out=k[:])
         centred = sb.tile([P, SLOTS], F32, name="centred", align_bytes=64)
-        nc.vector.scalar_tensor_tensor(centred[:], c_ext[:, :SLOTS], cbar[:], u[:, :SLOTS], ALU.subtract, ALU.mult)
+        nc.vector.scalar_tensor_tensor(centred[:], c_ext[:, :SLOTS], cbar[:], u[:, :SLOTS], ALU.add, ALU.mult)
+        row_scale = sb.tile([P, 1], F32, name="row_scale", tag="vals2_bf16", align_bytes=64)
+        nc.scalar.activation(row_scale[:], rz[:], ACT.Copy, scale=-1024.0)
         shift = sb.tile([P, SLOTS], F32, name="shift", align_bytes=64)
-        nc.scalar.activation(shift[:], s[:, :SLOTS], ACT.Copy, scale=k[:])
+        nc.scalar.activation(shift[:], p, ACT.Copy, scale=k[:])
         nc.vector.tensor_tensor(placed[:].indirect(offsets[:]), centred[:], shift[:], ALU.add)
 
         for n in range(T // STORE_COLS):
             cols = slice(n * STORE_COLS, (n + 1) * STORE_COLS)
             result = sb.tile([P, STORE_COLS], F32, name="result%d" % n, align_bytes=64)
-            nc.vector.scalar_tensor_tensor(result[:], placed[:, cols], 1024.0, base_sb[:, cols], ALU.mult, ALU.add)
+            nc.vector.scalar_tensor_tensor(result[:], placed[:, cols], row_scale[:], base_sb[:, cols], ALU.mult, ALU.add)
             queue = nc.sync if n % 2 == 0 else nc.scalar
             queue.dma_start(out=out[:, cols], in_=result[:])

from contextlib import ExitStack

import concourse.mybir as mybir

D, E, T, Q, SLOTS = 512, 512, 1024, 128, 256
FLOPS = 3 * 2 * 512 * Q * T

F32 = mybir.dt.float32
BF16 = mybir.dt.bfloat16
I32 = mybir.dt.int32
U32 = mybir.dt.uint32
U16 = mybir.dt.uint16
U8 = mybir.dt.uint8
FP8X4 = mybir.dt.float8_e4m3fn_x4
ALU = mybir.AluOpType
ACT = mybir.ActivationFunctionType

P = 128
PACK = 4
BANK = 512
PAD = 8
VALS_LOADS = (512, 384, 128)
VALS_PASSES = ((0, 0, 512, 256), (1, 256, 128, 128), (1, 0, 256, 0), (2, 0, 128, 128))
STORE_COLS = 256


def tile_attend_hvsharedprefix_heads_kernel(tc, query, keys_words, keys_scales, gout, vals, zp, cp, dquery, base, offs, out):
    nc = tc.nc
    with ExitStack() as ctx:
        sb = ctx.enter_context(tc.tile_pool(name="sb", bufs=1))
        ps = ctx.enter_context(tc.psum_pool(name="ps", bufs=1))

        def load_rows(name, rows):
            raw = sb.tile([P, PACK, rows.shape[1]], F32, name=name + "_raw", align_bytes=64)
            nc.sync.dma_start(out=raw[:], in_=rows.rearrange("(p j) w -> p j w", j=PACK))
            return raw

        def interleave(copy, grouped, raw):
            copy(grouped.rearrange("p (c i j) -> p c j i", i=4, j=PACK), raw.rearrange("p j (c i) -> p c j i", i=4))

        def round_to_bf16(name, raw, first, width, scalar_cols):
            grouped = sb.tile([P, width * PACK], BF16, name=name + "_bf16", align_bytes=64)
            split = width - scalar_cols
            if split > 0:
                interleave(nc.vector.tensor_copy, grouped[:, : split * PACK], raw[:, :, first : first + split])
            if scalar_cols > 0:
                interleave(nc.scalar.copy, grouped[:, split * PACK :], raw[:, :, first + split : first + width])
            return grouped

        def quantise(name, grouped):
            width = grouped.shape[1] // PACK
            codes = sb.tile([P, width], U32, name=name + "_codes", align_bytes=64)
            scales = sb.tile([P, width], U8, name=name + "_scales", align_bytes=64)
            nc.vector.quantize_mx(out=codes[:].bitcast(FP8X4), scales=scales[:], in_=grouped[:])
            return codes, scales

        def product(name, lhs, rhs, cols):
            bank = ps.tile([P, BANK], F32, name=name)
            width = cols.stop - cols.start
            nc.tensor.matmul_mx(
                out=bank[:, :width],
                lhsT=lhs[0][:].bitcast(FP8X4),
                lhsT_scale=lhs[1][:],
                rhs=rhs[0][:, cols].bitcast(FP8X4),
                rhs_scale=rhs[1][:, cols],
                start=True,
                stop=True,
            )
            return bank[:, :width]

        key_codes = sb.tile([P, T], U32, name="key_codes", align_bytes=64)
        key_scales = sb.tile([P, T], U8, name="key_scales", align_bytes=64)
        offsets = sb.tile([P, SLOTS // 16], U16, name="offsets")
        p_ext = sb.tile([P, PAD + SLOTS + PAD], F32, name="p_ext", align_bytes=64)
        t_ext = sb.tile([P, SLOTS + PAD], F32, name="t_ext", align_bytes=64)
        c_ext = sb.tile([P, SLOTS + PAD], F32, name="c_ext", align_bytes=64)
        placed = sb.tile([P, T], F32, name="placed", align_bytes=64)

        nc.vector.memset(key_scales[:].bitcast(I32), 0)
        nc.vector.memset(t_ext[:, SLOTS : SLOTS + 1], 0.0)
        nc.scalar.activation(c_ext[:, SLOTS : SLOTS + 1], t_ext[:, SLOTS : SLOTS + 1], ACT.Exp)
        nc.vector.memset(placed[:], 0.0)

        query_raw = load_rows("query", query)
        for r in range(4):
            nc.sync.dma_start(out=key_scales[r:P:32, :].bitcast(I32), in_=keys_scales[0, r:16:4, :].bitcast(I32))
        nc.sync.dma_start(out=key_codes[:].bitcast(I32), in_=keys_words[0].rearrange("p n t -> p (n t)").bitcast(I32))
        dquery_raw = load_rows("dquery", dquery)
        gout_raw = load_rows("gout", gout)
        nc.sync.dma_start(offsets[:], offs)
        nc.sync.dma_start(out=p_ext[:, PAD - 1 : PAD], in_=zp)
        nc.sync.dma_start(out=p_ext[:, PAD + SLOTS : PAD + SLOTS + 1], in_=cp)
        vals_raw = []
        start = 0
        for n, width in enumerate(VALS_LOADS):
            vals_raw.append(load_rows("vals%d" % n, vals[:, start : start + width]))
            start += width
        base_sb = sb.tile([P, T], F32, name="base_sb", align_bytes=64)
        nc.sync.dma_start(out=base_sb[:], in_=base)

        keys = (key_codes, key_scales)
        halves = [slice(0, BANK), slice(BANK, T)]
        a_sb = sb.tile([P, T], F32, name="a_sb", align_bytes=64)
        ta_sb = sb.tile([P, T], F32, name="ta_sb", align_bytes=64)

        query_mx = quantise("query", round_to_bf16("query", query_raw, 0, Q, 0))
        dquery_mx = quantise("dquery", round_to_bf16("dquery", dquery_raw, 0, Q, 0))
        a_banks = [product("a%d" % h, query_mx, keys, halves[h]) for h in range(2)]
        ta_banks = [product("ta%d" % h, dquery_mx, keys, halves[h]) for h in range(2)]
        gout_mx = quantise("gout", round_to_bf16("gout", gout_raw, 0, Q, 0))
        nc.scalar.copy(a_sb[:, halves[0]], a_banks[0])
        nc.scalar.copy(a_sb[:, halves[1]], a_banks[1])
        p = p_ext[:, PAD : PAD + SLOTS]
        nc.scalar.activation(p, a_sb[:].indirect(offsets[:]), ACT.Exp)
        nc.vector.tensor_copy(ta_sb[:, halves[0]], ta_banks[0])
        nc.vector.tensor_copy(ta_sb[:, halves[1]], ta_banks[1])

        z = sb.tile([P, 1], F32, name="z")
        z_terms = sb.tile([P, SLOTS + 1], F32, name="z_terms")
        nc.scalar.activation(z_terms[:], p_ext[:, PAD - 1 : PAD + SLOTS], ACT.Copy, scale=-1.0, accum_out=z[:])
        s = p_ext[:, PAD : PAD + SLOTS + 1]

        c_banks = []
        for n, (load, first, width, scalar_cols) in enumerate(VALS_PASSES):
            grouped = round_to_bf16("vals%d" % n, vals_raw[load], first, width, scalar_cols)
            if n == 0:
                nc.vector.tensor_copy(t_ext[:, :SLOTS], ta_sb[:].indirect(offsets[:]))
            vals_mx = quantise("vals%d" % n, grouped)
            c_banks.append(product("c%d" % n, gout_mx, vals_mx, slice(0, width)))
        c_sb = sb.tile([P, T], F32, name="c_sb", tag="vals2_raw", align_bytes=64)
        for bank, (load, first, width, scalar_cols) in zip(c_banks, VALS_PASSES):
            start = sum(VALS_LOADS[:load]) + first
            nc.scalar.copy(c_sb[:, start : start + width], bank)

        rz = sb.tile([P, 1], F32, name="rz", tag="vals0_bf16", align_bytes=64)
        nc.vector.reciprocal(rz[:], z[:])
        tbar = sb.tile([P, 1], F32, name="tbar")
        tbar_terms = sb.tile([P, SLOTS], F32, name="tbar_terms")
        nc.vector.scalar_tensor_tensor(tbar_terms[:], t_ext[:, :SLOTS], rz[:], p, ALU.mult, ALU.mult, accum_out=tbar[:])
        u = sb.tile([P, SLOTS + 1], F32, name="u", tag="vals3_bf16", align_bytes=64)
        nc.vector.scalar_tensor_tensor(u[:], t_ext[:, : SLOTS + 1], tbar[:], s, ALU.add, ALU.mult)
        nc.vector.tensor_copy(c_ext[:, :SLOTS], c_sb[:].indirect(offsets[:]))
        cbar = sb.tile([P, 1], F32, name="cbar")
        cbar_terms = sb.tile([P, SLOTS + 1], F32, name="cbar_terms")
        nc.vector.scalar_tensor_tensor(cbar_terms[:], c_ext[:, : SLOTS + 1], rz[:], s, ALU.mult, ALU.mult, accum_out=cbar[:])
        k = sb.tile([P, 1], F32, name="k")
        k_terms = sb.tile([P, SLOTS + 1], F32, name="k_terms")
        nc.vector.scalar_tensor_tensor(k_terms[:], c_ext[:, : SLOTS + 1], rz[:], u[:], ALU.mult, ALU.mult, accum_out=k[:])
        centred = sb.tile([P, SLOTS], F32, name="centred", align_bytes=64)
        nc.vector.scalar_tensor_tensor(centred[:], c_ext[:, :SLOTS], cbar[:], u[:, :SLOTS], ALU.add, ALU.mult)
        row_scale = sb.tile([P, 1], F32, name="row_scale", tag="vals2_bf16", align_bytes=64)
        nc.scalar.activation(row_scale[:], rz[:], ACT.Copy, scale=-1024.0)
        shift = sb.tile([P, SLOTS], F32, name="shift", align_bytes=64)
        nc.scalar.activation(shift[:], p, ACT.Copy, scale=k[:])
        nc.vector.tensor_tensor(placed[:].indirect(offsets[:]), centred[:], shift[:], ALU.add)

        for n in range(T // STORE_COLS):
            cols = slice(n * STORE_COLS, (n + 1) * STORE_COLS)
            result = sb.tile([P, STORE_COLS], F32, name="result%d" % n, align_bytes=64)
            nc.vector.scalar_tensor_tensor(result[:], placed[:, cols], row_scale[:], base_sb[:, cols], ALU.mult, ALU.add)
            queue = nc.sync if n % 2 == 0 else nc.scalar
            queue.dma_start(out=out[:, cols], in_=result[:])
